import numpy as np
import ml_dtypes


def mxq(x, axis, fmt="e4m3"):
    dtype, down = {"e4m3": (ml_dtypes.float8_e4m3fn, 7), "e5m2": (ml_dtypes.float8_e5m2, 14)}[fmt]
    v = np.moveaxis(np.asarray(x, np.float32).astype(ml_dtypes.bfloat16).astype(np.float64), axis, -1)
    blocks = v.reshape(v.shape[:-1] + (-1, 32))
    amax = np.abs(blocks).max(-1, keepdims=True)
    byte = np.maximum(np.where(amax > 0, np.frexp(amax)[1] - 1 + 127, 0) - down, 1)
    scale = np.exp2(byte - 127.0)
    codes = (blocks / scale).astype(np.float32).astype(dtype).astype(np.float64)
    return np.moveaxis((codes * scale).reshape(v.shape), -1, axis)


WIDE = False


def mx_kscale(k):
    if not WIDE:
        return np.ones(k)
    levels = np.array([30, -30])
    if k % 512:
        return np.exp2(np.random.permutation(np.resize(levels, k // 32))).repeat(32)
    a = np.empty((k // 512, 16))
    for p in range(k // 512):
        a[p, :8] = np.random.permutation(np.resize(levels, 8))
        for g in range(8):
            far = levels[np.abs(levels - a[p, g]) >= 10]
            a[p, g + 8] = far[np.random.randint(len(far))]
    return np.exp2(a.ravel()).repeat(32)


def f64(x):
    return np.asarray(x).astype(np.float64)


def striped(idx):
    return np.tile(np.asarray(idx).reshape(-1, 16).T, (8, 1)).astype(np.uint16)


def unstriped(offs):
    return offs[:16].T.reshape(-1).astype(np.int64)


E2M1 = np.array([0.0, 0.5, 1.0, 1.5, 2.0, 3.0, 4.0, 6.0, -0.0, -0.5, -1.0, -1.5, -2.0, -3.0, -4.0, -6.0])


def pack_weight(w, fmt):
    k, n = w.shape
    w = f64(np.asarray(w, np.float32).astype(ml_dtypes.bfloat16)).reshape(k // 32, 32, n)
    amax = np.abs(w).max(1)
    if fmt in ("e4m3", "e5m2"):
        byte = np.frexp(amax)[1] - 1 + 127 - (7 if fmt == "e4m3" else 14)
    else:
        mant, ex = np.frexp(amax / 6.0)
        byte = np.where(mant > 0.5, ex, ex - 1) + 127
    byte = np.clip(np.where(amax > 0, byte, 1), 1, 254)
    scaled = (w * np.exp2(127.0 - byte)[:, None, :]).reshape(k, n).astype(np.float32)
    by_word = np.ascontiguousarray(scaled.reshape(k // 512, 128, 4, n).transpose(0, 1, 3, 2))
    if fmt in ("e4m3", "e5m2"):
        words = by_word.astype(ml_dtypes.float8_e4m3fn if fmt == "e4m3" else ml_dtypes.float8_e5m2).view(np.uint8)
    else:
        c = by_word.astype(ml_dtypes.float4_e2m1fn).view(np.uint8) & 0xF
        words = (c[..., 0::2] | (c[..., 1::2] << 4)).reshape(k // 512, 128, 2 * n)
    return np.ascontiguousarray(words), np.ascontiguousarray(byte.astype(np.uint8).reshape(k // 512, 16, n))


def unpack_weight(words, scales, fmt):
    g, _, n = scales.shape
    words = np.ascontiguousarray(words).reshape(g, 128, n, -1)
    if fmt in ("e4m3", "e5m2"):
        vals = words.view(ml_dtypes.float8_e4m3fn if fmt == "e4m3" else ml_dtypes.float8_e5m2).astype(np.float64)
    else:
        nib = np.empty((g, 128, n, 4), np.uint8)
        nib[..., 0::2] = words & 0xF
        nib[..., 1::2] = words >> 4
        vals = E2M1[nib]
    vals = vals * np.repeat(np.exp2(scales.astype(np.float64) - 127.0), 8, axis=1)[..., None]
    return vals.transpose(0, 1, 3, 2).reshape(g * 512, n)


K, J, N, R, T = 512, 512, 256, 256, 1024


def setup_inputs():
    n = np.random.standard_normal
    idx = np.random.permutation(T)[:J]
    idx2 = np.random.permutation(T)[:J]
    fj = mx_kscale(J)
    fk = mx_kscale(K)
    gjp = pack_weight(n((J, N)) * np.exp(0.5 * n((J, 1))) / fj[:, None], "e5m2")
    drp = pack_weight(n((K, R)) * 1 / np.sqrt(K) / fk[:, None], "e4m3")
    return {
        "xf": (n((K, T))).astype(np.float32),
        "ra": (np.random.uniform(0.5, 1.5, (1, J)) * fj).astype(np.float32),
        "gj_words": gjp[0],
        "gj_scales": gjp[1],
        "fkr": (np.random.uniform(0.5, 1.5, (1, K)) * fk).astype(np.float32),
        "dr_words": drp[0],
        "dr_scales": drp[1],
        "bn": (np.random.uniform(-12.0, 12.0, (1, N))).astype(np.float32),
        "offs": striped(idx),
        "offs2": striped(idx2),
    }


def reference(xf, ra, gj_words, gj_scales, fkr, dr_words, dr_scales, bn, offs, offs2):
    idx = unstriped(offs)
    idx2 = unstriped(offs2)
    gju = unpack_weight(gj_words, gj_scales, "e5m2")
    dru = unpack_weight(dr_words, dr_scales, "e4m3")
    us = np.maximum(f64(xf)[:, idx], f64(xf)[:, idx2]) * f64(ra)
    ut = us.T
    uj = ut * f64(fkr)
    ujq = mxq(uj, 0, "e4m3")
    w = ujq.T @ gju
    wq = mxq(w, 0, "e5m2")
    v2 = dru.T @ wq
    wv = v2 + f64(bn)
    mn = np.mean(wv, axis=1, keepdims=True)
    dw = wv - mn
    y = dw / (np.mean(np.abs(dw), axis=1, keepdims=True) + 2.0)
    return y

@@ -1,0 +1,196 @@
+from contextlib import ExitStack
+
+import concourse.mybir as mybir
+from concourse.masks import make_identity
+
+K, J, N, R, T = 512, 512, 256, 256, 1024
+FLOPS = 2 * J * K * N + 2 * K * R * N
+
+F32 = mybir.dt.float32
+BF16 = mybir.dt.bfloat16
+I32 = mybir.dt.int32
+U32 = mybir.dt.uint32
+U16 = mybir.dt.uint16
+U8 = mybir.dt.uint8
+E4M3 = mybir.dt.float8_e4m3fn_x4
+E5M2 = mybir.dt.float8_e5m2_x4
+ALU = mybir.AluOpType
+ACT = mybir.ActivationFunctionType
+
+P = 128
+PACK = 4
+LIST_ROWS = 16
+VECTOR_SLOTS = (512, 512, 256)
+
+
+def tile_list_directions_larger_stored_spread_kernel(
+    tc, xf, ra, gj_words, gj_scales, fkr, dr_words, dr_scales, bn, offs, offs2, out
+):
+    nc = tc.nc
+    with ExitStack() as ctx:
+        keep = ctx.enter_context(tc.tile_pool(name="keep", bufs=1))
+        psum = ctx.enter_context(tc.psum_pool(name="psum", bufs=1))
+
+        list_a = keep.tile([P, J // LIST_ROWS], U16, name="list_a")
+        list_b = keep.tile([P, J // LIST_ROWS], U16, name="list_b")
+        xf_planes = xf.rearrange("(p t) c -> p t c", t=PACK)
+        planes = [keep.tile([P, T], F32, name="plane%d" % t) for t in range(PACK)]
+        nc.sync.dma_start(planes[0][:], xf_planes[:, 0, :])
+        nc.sync.dma_start(list_a[:], offs)
+        nc.sync.dma_start(list_b[:], offs2)
+
+        ra4 = keep.tile([P, PACK], F32, name="ra4")
+        fk4 = keep.tile([P, PACK], F32, name="fk4")
+        nc.sync.dma_start(planes[1][:], xf_planes[:, 1, :])
+        nc.sync.dma_start(ra4[:], ra.rearrange("o (q i) -> (o q) i", i=PACK))
+        nc.sync.dma_start(fk4[:], fkr.rearrange("o (p t) -> (o p) t", t=PACK))
+
+        for t in range(2, PACK):
+            nc.sync.dma_start(planes[t][:], xf_planes[:, t, :])
+
+        gj_codes = keep.tile([P, N], U32, name="gj_codes", align_bytes=64)
+        dr_codes = keep.tile([P, R], U32, name="dr_codes", align_bytes=64)
+        gj_sc = keep.tile([P, N], U8, name="gj_sc", align_bytes=64)
+        dr_sc = keep.tile([P, R], U8, name="dr_sc", align_bytes=64)
+        bn_all = keep.tile([P, N], F32, name="bn_all")
+        nc.gpsimd.memset(gj_sc[:].bitcast(U32), 0)
+        nc.gpsimd.memset(dr_sc[:].bitcast(U32), 0)
+        ident = keep.tile([P, P], F32, name="ident")
+        make_identity(nc, ident[:])
+
+        nc.sync.dma_start(gj_codes[:].bitcast(I32), gj_words[0].rearrange("p n t -> p (n t)").bitcast(I32))
+        nc.sync.dma_start(dr_codes[:].bitcast(I32), dr_words[0].rearrange("p n t -> p (n t)").bitcast(I32))
+        for sc_tile, sc_in in ((gj_sc, gj_scales), (dr_sc, dr_scales)):
+            for quad in range(4):
+                nc.sync.dma_start(
+                    sc_tile[32 * quad : 32 * quad + 4, :].bitcast(I32),
+                    sc_in[0, 4 * quad : 4 * quad + 4, :].bitcast(I32),
+                )
+        nc.sync.dma_start(bn_all[:], bn[0].partition_broadcast(P))
+
+        ra_ps = psum.tile([P, PACK, P], F32, name="ra_ps")
+        for i in range(PACK):
+            nc.tensor.transpose(ra_ps[:, i, :], ra4[:, i : i + 1].to_broadcast([P, P]), ident[:])
+        ra_by_slot = ra_ps[:].rearrange("p i q -> p q i")
+
+        def gather(on_vector, dst, plane, offsets, lo, hi):
+            picked = plane[:].indirect(offsets[:, lo // LIST_ROWS : hi // LIST_ROWS])
+            if on_vector:
+                nc.vector.tensor_copy(dst, picked)
+            else:
+                nc.scalar.activation(dst, picked, ACT.Copy)
+
+        turned = [
+            psum.tile([P, 2, 2, P], F32, name="turned01"),
+            psum.tile([P, 1, 2, P], F32, name="turned2"),
+            psum.tile([P, 1, 2, P], F32, name="turned3"),
+        ]
+        turned_of = [turned[0][:, 0], turned[0][:, 1], turned[1][:, 0], turned[2][:, 0]]
+
+        for t in range(PACK):
+            last = t == PACK - 1
+            a_vals = keep.tile([P, J], F32, name="a%d" % t, align_bytes=64)
+            b_vals = keep.tile([P, J], F32, name="b%d" % t, align_bytes=64)
+            larger = keep.tile([P, J], F32, name="m%d" % t, tag="larger", bufs=2, align_bytes=64)
+            cuts = (0, 256, 384, 512) if last else (0, 256, 512)
+            pieces = list(zip(cuts[:-1], cuts[1:]))
+            if last:
+                a_head = keep.tile([P, cuts[1]], F32, name="a_head", tag="held", align_bytes=64)
+                a_parts = [a_head[:]] + [a_vals[:, lo:hi] for lo, hi in pieces[1:]]
+                for s, (lo, hi) in enumerate(pieces):
+                    gather(False, a_parts[s], planes[t], list_a, lo, hi)
+                    gather(False, b_vals[:, lo:hi], planes[t], list_b, lo, hi)
+            else:
+                a_parts = [a_vals[:, lo:hi] for lo, hi in pieces]
+                for lo, hi in pieces:
+                    gather(False, a_vals[:, lo:hi], planes[t], list_a, lo, hi)
+                for lo, hi in pieces:
+                    gather(hi <= VECTOR_SLOTS[t], b_vals[:, lo:hi], planes[t], list_b, lo, hi)
+            uj_bf = keep.tile([P, J], BF16, name="uj_bf%d" % t, align_bytes=64)
+            for s, (lo, hi) in enumerate(pieces):
+                nc.vector.tensor_tensor(larger[:, lo:hi], a_parts[s], b_vals[:, lo:hi], ALU.max)
+            for s, (lo, hi) in enumerate(pieces):
+                nc.vector.scalar_tensor_tensor(
+                    uj_bf[:, lo:hi].rearrange("p (q i) -> p q i", i=PACK),
+                    larger[:, lo:hi].rearrange("p (q i) -> p q i", i=PACK),
+                    fk4[:, t : t + 1],
+                    ra_by_slot[:, lo // PACK : hi // PACK, :],
+                    ALU.mult,
+                    ALU.mult,
+                )
+            pairs = uj_bf[:].bitcast(F32)
+            for u in range(2):
+                nc.tensor.transpose(turned_of[t][:, u, :], pairs[:, u::2], ident[:])
+
+        w_ps = [psum.tile([P, PACK, P], F32, name="w_ps%d" % h) for h in range(2)]
+        early = keep.tile([P, 3, P * PACK], BF16, name="early", tag="held", align_bytes=64)
+        late = keep.tile([P, 1, P * PACK], BF16, name="late", align_bytes=64)
+        groups = [(turned[0], early[:, 0:2, :], (0, 1)), (turned[1], early[:, 2:3, :], (2,)), (turned[2], late[:], (3,))]
+        for g, (src, grouped, ts) in enumerate(groups):
+            nc.scalar.copy(
+                grouped.bitcast(F32).rearrange("p t (k u) -> p t k u", u=2),
+                src[:].rearrange("p t u k -> p t k u"),
+            )
+            uj_codes = keep.tile([P, len(ts) * P], U32, name="uj_codes%d" % g, align_bytes=64)
+            uj_sc = keep.tile([P, len(ts) * P], U8, name="uj_sc%d" % g, align_bytes=64)
+            nc.vector.quantize_mx(
+                out=uj_codes[:].bitcast(E4M3), scales=uj_sc[:], in_=grouped.rearrange("p t c -> p (t c)")
+            )
+            for x, t in enumerate(ts):
+                cols = slice(x * P, (x + 1) * P)
+                for h in range(2):
+                    n_cols = slice(h * P, (h + 1) * P)
+                    nc.tensor.matmul_mx(
+                        out=w_ps[h][:, t, :],
+                        lhsT=uj_codes[:, cols].bitcast(E4M3),
+                        lhsT_scale=uj_sc[:, cols],
+                        rhs=gj_codes[:, n_cols].bitcast(E5M2),
+                        rhs_scale=gj_sc[:, n_cols],
+                        start=True,
+                        stop=True,
+                    )
+
+        v_ps = [psum.tile([P, N], F32, name="v_ps%d" % g) for g in range(2)]
+        w_bf = [keep.tile([P, P, PACK], BF16, name="w_bf%d" % h, align_bytes=64) for h in range(2)]
+        nc.scalar.copy(w_bf[0][:], w_ps[0][:].rearrange("p t n -> p n t"))
+        nc.vector.tensor_copy(w_bf[1][:], w_ps[1][:].rearrange("p t n -> p n t"))
+        for h in range(2):
+            w_codes = keep.tile([P, P], U32, name="w_codes%d" % h, align_bytes=64)
+            w_sc = keep.tile([P, P], U8, name="w_sc%d" % h, align_bytes=64)
+            nc.vector.quantize_mx(
+                out=w_codes[:].bitcast(E5M2), scales=w_sc[:], in_=w_bf[h][:].rearrange("p n t -> p (n t)")
+            )
+            for g in range(2):
+                r_cols = slice(g * P, (g + 1) * P)
+                nc.tensor.matmul_mx(
+                    out=v_ps[g][:, h * P : (h + 1) * P],
+                    lhsT=dr_codes[:, r_cols].bitcast(E4M3),
+                    lhsT_scale=dr_sc[:, r_cols],
+                    rhs=w_codes[:].bitcast(E5M2),
+                    rhs_scale=w_sc[:],
+                    start=True,
+                    stop=True,
+                )
+
+        abs_sum = keep.tile([P, 2], F32, name="abs_sum")
+        den = keep.tile([P, 2], F32, name="den")
+        inv = keep.tile([P, 2], F32, name="inv")
+        dev = []
+        for g in range(2):
+            wv = keep.tile([P, N], F32, name="wv%d" % g)
+            row_sum = keep.tile([P, 1], F32, name="row_sum%d" % g)
+            dev_abs = keep.tile([P, N], F32, name="dev_abs%d" % g)
+            dev.append(keep.tile([P, N], F32, name="dev%d" % g))
+            nc.vector.scalar_tensor_tensor(
+                wv[:], v_ps[g][:], 1.0, bn_all[:], ALU.mult, ALU.add, accum_out=row_sum[:]
+            )
+            nc.scalar.activation(
+                dev_abs[:], wv[:], ACT.Abs, bias=row_sum[:], scale=-float(N), accum_out=abs_sum[:, g : g + 1]
+            )
+            nc.vector.tensor_scalar(dev[g][:], wv[:], float(N), row_sum[:], ALU.mult, ALU.subtract)
+        nc.vector.tensor_scalar(den[:], abs_sum[:], 1.0 / N, 2.0 * N, ALU.mult, ALU.add)
+        nc.vector.reciprocal(inv[:], den[:])
+        for g in range(2):
+            res = keep.tile([P, N], F32, name="res%d" % g)
+            nc.vector.tensor_scalar(res[:], dev[g][:], inv[:, g : g + 1], None, ALU.mult)
+            nc.sync.dma_start(out[g * P : (g + 1) * P, :], res[:])

@@ -45,6 +45,11 @@ def tile_list_directions_larger_stored_spread_kernel(
         nc.sync.dma_start(ra4[:], ra.rearrange("o (q i) -> (o q) i", i=PACK))
         nc.sync.dma_start(fk4[:], fkr.rearrange("o (p t) -> (o p) t", t=PACK))
 
+        warm_in = keep.tile([P, 1], F32, name="warm_in")
+        warm_out = keep.tile([P, 1], F32, name="warm_out")
+        nc.vector.memset(warm_in[:], 0.0)
+        nc.scalar.activation(warm_out[:], warm_in[:], ACT.Abs)
+
         for t in range(2, PACK):
             nc.sync.dma_start(planes[t][:], xf_planes[:, t, :])
 

@@ -20,7 +20,7 @@ ACT = mybir.ActivationFunctionType
 P = 128
 PACK = 4
 LIST_ROWS = 16
-VECTOR_SLOTS = (512, 512, 256)
+VECTOR_SLOTS = (512, 512, 128)
 
 
 def tile_list_directions_larger_stored_spread_kernel(
@@ -109,7 +109,8 @@ def tile_list_directions_larger_stored_spread_kernel(
                 a_parts = [a_vals[:, lo:hi] for lo, hi in pieces]
                 for lo, hi in pieces:
                     gather(False, a_vals[:, lo:hi], planes[t], list_a, lo, hi)
-                for lo, hi in pieces:
+                b_cuts = cuts if VECTOR_SLOTS[t] == J else (0, VECTOR_SLOTS[t], J)
+                for lo, hi in zip(b_cuts[:-1], b_cuts[1:]):
                     gather(hi <= VECTOR_SLOTS[t], b_vals[:, lo:hi], planes[t], list_b, lo, hi)
             uj_bf = keep.tile([P, J], BF16, name="uj_bf%d" % t, align_bytes=64)
             for s, (lo, hi) in enumerate(pieces):
@@ -197,5 +198,9 @@ def tile_list_directions_larger_stored_spread_kernel(
         nc.vector.reciprocal(inv[:], den[:])
         for g in range(2):
             res = keep.tile([P, N], F32, name="res%d" % g)
-            nc.vector.tensor_scalar(res[:], dev[g][:], inv[:, g : g + 1], None, ALU.mult)
-            nc.sync.dma_start(out[g * P : (g + 1) * P, :], res[:])
+            if g == 0:
+                nc.vector.tensor_scalar(res[:], dev[g][:], inv[:, g : g + 1], None, ALU.mult)
+                nc.sync.dma_start(out[g * P : (g + 1) * P, :], res[:])
+            else:
+                nc.scalar.activation(res[:], dev[g][:], ACT.Copy, scale=inv[:, g : g + 1])
+                nc.scalar.dma_start(out[g * P : (g + 1) * P, :], res[:])

@@ -20,7 +20,7 @@ ACT = mybir.ActivationFunctionType
 P = 128
 PACK = 4
 LIST_ROWS = 16
-VECTOR_SLOTS = (512, 512, 128)
+VECTOR_SLOTS = (512, 512, 256, 256)
 
 
 def tile_list_directions_larger_stored_spread_kernel(
@@ -104,10 +104,10 @@ def tile_list_directions_larger_stored_spread_kernel(
                 a_parts = [a_head[:]] + [a_vals[:, lo:hi] for lo, hi in pieces[1:]]
                 for s, (lo, hi) in enumerate(pieces):
                     gather(False, a_parts[s], planes[t], list_a, lo, hi)
-                    gather(False, b_vals[:, lo:hi], planes[t], list_b, lo, hi)
+                    gather(hi <= VECTOR_SLOTS[t], b_vals[:, lo:hi], planes[t], list_b, lo, hi)
             else:
                 a_parts = [a_vals[:, lo:hi] for lo, hi in pieces]
-                for lo, hi in pieces:
+                for lo, hi in pieces if t == 0 else [(0, J)]:
                     gather(False, a_vals[:, lo:hi], planes[t], list_a, lo, hi)
                 b_cuts = cuts if VECTOR_SLOTS[t] == J else (0, VECTOR_SLOTS[t], J)
                 for lo, hi in zip(b_cuts[:-1], b_cuts[1:]):

@@ -20,7 +20,7 @@ ACT = mybir.ActivationFunctionType
 P = 128
 PACK = 4
 LIST_ROWS = 16
-VECTOR_SLOTS = (512, 512, 256, 256)
+VECTOR_SLOTS = (512, 512, 128, 256)
 
 
 def tile_list_directions_larger_stored_spread_kernel(
@@ -97,7 +97,7 @@ def tile_list_directions_larger_stored_spread_kernel(
             a_vals = keep.tile([P, J], F32, name="a%d" % t, align_bytes=64)
             b_vals = keep.tile([P, J], F32, name="b%d" % t, align_bytes=64)
             larger = keep.tile([P, J], F32, name="m%d" % t, tag="larger", bufs=2, align_bytes=64)
-            cuts = (0, 256, 384, 512) if last else (0, 256, 512)
+            cuts = (0, 256, 448, 512) if last else (0, 256, 512)
             pieces = list(zip(cuts[:-1], cuts[1:]))
             if last:
                 a_head = keep.tile([P, cuts[1]], F32, name="a_head", tag="held", align_bytes=64)

from contextlib import ExitStack

import concourse.mybir as mybir
from concourse.masks import make_identity

K, J, N, R, T = 512, 512, 256, 256, 1024
FLOPS = 2 * J * K * N + 2 * K * R * N

F32 = mybir.dt.float32
BF16 = mybir.dt.bfloat16
I32 = mybir.dt.int32
U32 = mybir.dt.uint32
U16 = mybir.dt.uint16
U8 = mybir.dt.uint8
E4M3 = mybir.dt.float8_e4m3fn_x4
E5M2 = mybir.dt.float8_e5m2_x4
ALU = mybir.AluOpType
ACT = mybir.ActivationFunctionType

P = 128
PACK = 4
LIST_ROWS = 16
VECTOR_SLOTS = (512, 512, 128, 256)


def tile_list_directions_larger_stored_spread_kernel(
    tc, xf, ra, gj_words, gj_scales, fkr, dr_words, dr_scales, bn, offs, offs2, out
):
    nc = tc.nc
    with ExitStack() as ctx:
        keep = ctx.enter_context(tc.tile_pool(name="keep", bufs=1))
        psum = ctx.enter_context(tc.psum_pool(name="psum", bufs=1))

        list_a = keep.tile([P, J // LIST_ROWS], U16, name="list_a")
        list_b = keep.tile([P, J // LIST_ROWS], U16, name="list_b")
        xf_planes = xf.rearrange("(p t) c -> p t c", t=PACK)
        planes = [keep.tile([P, T], F32, name="plane%d" % t) for t in range(PACK)]
        nc.sync.dma_start(planes[0][:], xf_planes[:, 0, :])
        nc.sync.dma_start(list_a[:], offs)
        nc.sync.dma_start(list_b[:], offs2)

        ra4 = keep.tile([P, PACK], F32, name="ra4")
        fk4 = keep.tile([P, PACK], F32, name="fk4")
        nc.sync.dma_start(planes[1][:], xf_planes[:, 1, :])
        nc.sync.dma_start(ra4[:], ra.rearrange("o (q i) -> (o q) i", i=PACK))
        nc.sync.dma_start(fk4[:], fkr.rearrange("o (p t) -> (o p) t", t=PACK))

        warm_in = keep.tile([P, 1], F32, name="warm_in")
        warm_out = keep.tile([P, 1], F32, name="warm_out")
        nc.vector.memset(warm_in[:], 0.0)
        nc.scalar.activation(warm_out[:], warm_in[:], ACT.Abs)

        for t in range(2, PACK):
            nc.sync.dma_start(planes[t][:], xf_planes[:, t, :])

        gj_codes = keep.tile([P, N], U32, name="gj_codes", align_bytes=64)
        dr_codes = keep.tile([P, R], U32, name="dr_codes", align_bytes=64)
        gj_sc = keep.tile([P, N], U8, name="gj_sc", align_bytes=64)
        dr_sc = keep.tile([P, R], U8, name="dr_sc", align_bytes=64)
        bn_all = keep.tile([P, N], F32, name="bn_all")
        nc.gpsimd.memset(gj_sc[:].bitcast(U32), 0)
        nc.gpsimd.memset(dr_sc[:].bitcast(U32), 0)
        ident = keep.tile([P, P], F32, name="ident")
        make_identity(nc, ident[:])

        nc.sync.dma_start(gj_codes[:].bitcast(I32), gj_words[0].rearrange("p n t -> p (n t)").bitcast(I32))
        nc.sync.dma_start(dr_codes[:].bitcast(I32), dr_words[0].rearrange("p n t -> p (n t)").bitcast(I32))
        for sc_tile, sc_in in ((gj_sc, gj_scales), (dr_sc, dr_scales)):
            for quad in range(4):
                nc.sync.dma_start(
                    sc_tile[32 * quad : 32 * quad + 4, :].bitcast(I32),
                    sc_in[0, 4 * quad : 4 * quad + 4, :].bitcast(I32),
                )
        nc.sync.dma_start(bn_all[:], bn[0].partition_broadcast(P))

        ra_ps = psum.tile([P, PACK, P], F32, name="ra_ps")
        for i in range(PACK):
            nc.tensor.transpose(ra_ps[:, i, :], ra4[:, i : i + 1].to_broadcast([P, P]), ident[:])
        ra_by_slot = ra_ps[:].rearrange("p i q -> p q i")

        def gather(on_vector, dst, plane, offsets, lo, hi):
            picked = plane[:].indirect(offsets[:, lo // LIST_ROWS : hi // LIST_ROWS])
            if on_vector:
                nc.vector.tensor_copy(dst, picked)
            else:
                nc.scalar.activation(dst, picked, ACT.Copy)

        turned = [
            psum.tile([P, 2, 2, P], F32, name="turned01"),
            psum.tile([P, 1, 2, P], F32, name="turned2"),
            psum.tile([P, 1, 2, P], F32, name="turned3"),
        ]
        turned_of = [turned[0][:, 0], turned[0][:, 1], turned[1][:, 0], turned[2][:, 0]]

        for t in range(PACK):
            last = t == PACK - 1
            a_vals = keep.tile([P, J], F32, name="a%d" % t, align_bytes=64)
            b_vals = keep.tile([P, J], F32, name="b%d" % t, align_bytes=64)
            larger = keep.tile([P, J], F32, name="m%d" % t, tag="larger", bufs=2, align_bytes=64)
            cuts = (0, 256, 448, 512) if last else (0, 256, 512)
            pieces = list(zip(cuts[:-1], cuts[1:]))
            if last:
                a_head = keep.tile([P, cuts[1]], F32, name="a_head", tag="held", align_bytes=64)
                a_parts = [a_head[:]] + [a_vals[:, lo:hi] for lo, hi in pieces[1:]]
                for s, (lo, hi) in enumerate(pieces):
                    gather(False, a_parts[s], planes[t], list_a, lo, hi)
                    gather(hi <= VECTOR_SLOTS[t], b_vals[:, lo:hi], planes[t], list_b, lo, hi)
            else:
                a_parts = [a_vals[:, lo:hi] for lo, hi in pieces]
                for lo, hi in pieces if t == 0 else [(0, J)]:
                    gather(False, a_vals[:, lo:hi], planes[t], list_a, lo, hi)
                b_cuts = cuts if VECTOR_SLOTS[t] == J else (0, VECTOR_SLOTS[t], J)
                for lo, hi in zip(b_cuts[:-1], b_cuts[1:]):
                    gather(hi <= VECTOR_SLOTS[t], b_vals[:, lo:hi], planes[t], list_b, lo, hi)
            uj_bf = keep.tile([P, J], BF16, name="uj_bf%d" % t, align_bytes=64)
            for s, (lo, hi) in enumerate(pieces):
                nc.vector.tensor_tensor(larger[:, lo:hi], a_parts[s], b_vals[:, lo:hi], ALU.max)
            for s, (lo, hi) in enumerate(pieces):
                nc.vector.scalar_tensor_tensor(
                    uj_bf[:, lo:hi].rearrange("p (q i) -> p q i", i=PACK),
                    larger[:, lo:hi].rearrange("p (q i) -> p q i", i=PACK),
                    fk4[:, t : t + 1],
                    ra_by_slot[:, lo // PACK : hi // PACK, :],
                    ALU.mult,
                    ALU.mult,
                )
            pairs = uj_bf[:].bitcast(F32)
            for u in range(2):
                nc.tensor.transpose(turned_of[t][:, u, :], pairs[:, u::2], ident[:])

        w_ps = [psum.tile([P, PACK, P], F32, name="w_ps%d" % h) for h in range(2)]
        early = keep.tile([P, 3, P * PACK], BF16, name="early", tag="held", align_bytes=64)
        late = keep.tile([P, 1, P * PACK], BF16, name="late", align_bytes=64)
        groups = [(turned[0], early[:, 0:2, :], (0, 1)), (turned[1], early[:, 2:3, :], (2,)), (turned[2], late[:], (3,))]
        for g, (src, grouped, ts) in enumerate(groups):
            nc.scalar.copy(
                grouped.bitcast(F32).rearrange("p t (k u) -> p t k u", u=2),
                src[:].rearrange("p t u k -> p t k u"),
            )
            uj_codes = keep.tile([P, len(ts) * P], U32, name="uj_codes%d" % g, align_bytes=64)
            uj_sc = keep.tile([P, len(ts) * P], U8, name="uj_sc%d" % g, align_bytes=64)
            nc.vector.quantize_mx(
                out=uj_codes[:].bitcast(E4M3), scales=uj_sc[:], in_=grouped.rearrange("p t c -> p (t c)")
            )
            for x, t in enumerate(ts):
                cols = slice(x * P, (x + 1) * P)
                for h in range(2):
                    n_cols = slice(h * P, (h + 1) * P)
                    nc.tensor.matmul_mx(
                        out=w_ps[h][:, t, :],
                        lhsT=uj_codes[:, cols].bitcast(E4M3),
                        lhsT_scale=uj_sc[:, cols],
                        rhs=gj_codes[:, n_cols].bitcast(E5M2),
                        rhs_scale=gj_sc[:, n_cols],
                        start=True,
                        stop=True,
                    )

        v_ps = [psum.tile([P, N], F32, name="v_ps%d" % g) for g in range(2)]
        w_bf = [keep.tile([P, P, PACK], BF16, name="w_bf%d" % h, align_bytes=64) for h in range(2)]
        nc.scalar.copy(w_bf[0][:], w_ps[0][:].rearrange("p t n -> p n t"))
        nc.vector.tensor_copy(w_bf[1][:], w_ps[1][:].rearrange("p t n -> p n t"))
        for h in range(2):
            w_codes = keep.tile([P, P], U32, name="w_codes%d" % h, align_bytes=64)
            w_sc = keep.tile([P, P], U8, name="w_sc%d" % h, align_bytes=64)
            nc.vector.quantize_mx(
                out=w_codes[:].bitcast(E5M2), scales=w_sc[:], in_=w_bf[h][:].rearrange("p n t -> p (n t)")
            )
            for g in range(2):
                r_cols = slice(g * P, (g + 1) * P)
                nc.tensor.matmul_mx(
                    out=v_ps[g][:, h * P : (h + 1) * P],
                    lhsT=dr_codes[:, r_cols].bitcast(E4M3),
                    lhsT_scale=dr_sc[:, r_cols],
                    rhs=w_codes[:].bitcast(E5M2),
                    rhs_scale=w_sc[:],
                    start=True,
                    stop=True,
                )

        abs_sum = keep.tile([P, 2], F32, name="abs_sum")
        den = keep.tile([P, 2], F32, name="den")
        inv = keep.tile([P, 2], F32, name="inv")
        dev = []
        for g in range(2):
            wv = keep.tile([P, N], F32, name="wv%d" % g)
            row_sum = keep.tile([P, 1], F32, name="row_sum%d" % g)
            dev_abs = keep.tile([P, N], F32, name="dev_abs%d" % g)
            dev.append(keep.tile([P, N], F32, name="dev%d" % g))
            nc.vector.scalar_tensor_tensor(
                wv[:], v_ps[g][:], 1.0, bn_all[:], ALU.mult, ALU.add, accum_out=row_sum[:]
            )
            nc.scalar.activation(
                dev_abs[:], wv[:], ACT.Abs, bias=row_sum[:], scale=-float(N), accum_out=abs_sum[:, g : g + 1]
            )
            nc.vector.tensor_scalar(dev[g][:], wv[:], float(N), row_sum[:], ALU.mult, ALU.subtract)
        nc.vector.tensor_scalar(den[:], abs_sum[:], 1.0 / N, 2.0 * N, ALU.mult, ALU.add)
        nc.vector.reciprocal(inv[:], den[:])
        for g in range(2):
            res = keep.tile([P, N], F32, name="res%d" % g)
            if g == 0:
                nc.vector.tensor_scalar(res[:], dev[g][:], inv[:, g : g + 1], None, ALU.mult)
                nc.sync.dma_start(out[g * P : (g + 1) * P, :], res[:])
            else:
                nc.scalar.activation(res[:], dev[g][:], ACT.Copy, scale=inv[:, g : g + 1])
                nc.scalar.dma_start(out[g * P : (g + 1) * P, :], res[:])
